import numpy as np, ml_dtypes
CORES = [52,68,84,180,196,212,308,324,340]
N = 9
F, TK = 64, 64
def setup_inputs(rng):
    return {"x": rng.standard_normal((N, 128, N * TK), dtype=np.float32).astype(ml_dtypes.bfloat16), "w": rng.standard_normal((N, 128, F), dtype=np.float32).astype(ml_dtypes.bfloat16)}
def setup_inputs_big(rng):
    d = setup_inputs(rng)
    for k in ("x", "w"): d[k] = (d[k].astype(np.float32) * 1024.0).astype(d[k].dtype)
    return d
def setup_inputs_small(rng):
    d = setup_inputs(rng)
    for k in ("x", "w"): d[k] = (d[k].astype(np.float32) * (1 / 1024.0)).astype(d[k].dtype)
    return d
def setup_inputs_apart(rng):
    d = setup_inputs(rng)
    f = (10.0 ** rng.permutation(np.linspace(-1.5, 1.5, N))).astype(np.float32).reshape(N, 1, 1)
    for k in ("x", "w"): d[k] = (d[k].astype(np.float32) * f).astype(d[k].dtype)
    return d
def reference(x, w):
    X, W = x.astype(np.float64), w.astype(np.float64)
    y = np.zeros((N, F, N * TK))
    for r in range(N):
        for j in range(N):
            y[r][:, TK * j:TK * j + TK] = W[r].T @ X[j][:, TK * r:TK * r + TK]
    return {"y": y.astype(ml_dtypes.bfloat16 if x.dtype != np.float64 else np.float64)}

@@ -1,0 +1,187 @@
+from concourse.bass import DstId, RemoteDMATransfer
+
+B = 64
+F = 64
+NB = 9
+SLOT = 4
+
+SCRATCH = {
+    "xs": ("sbuf", [128, NB * B], "bfloat16"),
+    "ws": ("sbuf", [128, F], "bfloat16"),
+    "land": ("sbuf", [128, NB * B], "bfloat16"),
+    "fw0": ("sbuf", [128, SLOT * B], "bfloat16"),
+    "fw1": ("sbuf", [128, SLOT * B], "bfloat16"),
+    "rl": ("sbuf", [128, SLOT * B], "bfloat16"),
+    "yb": ("sbuf", [128, NB * B], "bfloat16"),
+    "ps0": ("psum", [128, 512], "float32"),
+    "ps1": ("psum", [128, 512], "float32"),
+    "ps2": ("psum", [128, 512], "float32"),
+    "ps3": ("psum", [128, 512], "float32"),
+}
+SEMAPHORES = ["ldx", "ldy", "ldw", "sent", "near", "far0", "far1", "f0", "f1", "rel",
+              "mm0", "mm1", "mm2", "mm3", "cp0", "cp1", "cp2", "cp3", "st0", "st1", "st2"]
+
+
+def _runs(items, key):
+    out = []
+    for it in items:
+        if out and key(it) == key(out[-1][-1]) + 1:
+            out[-1].append(it)
+        else:
+            out.append([it])
+    return out
+
+
+def _plan(cores, topo):
+    R = range(len(cores))
+
+    def ok(s, d):
+        return topo.may_write(cores[s], cores[d])
+
+    def near(s, d):
+        return topo.host(cores[s]) == topo.host(cores[d])
+
+    via = {}
+    for s in R:
+        for d in R:
+            if s != d and not ok(s, d):
+                via[s, d] = [m for m in R if m != s and m != d and ok(s, m) and ok(m, d)
+                             and topo.chip(cores[m]) == topo.chip(cores[d])][0]
+    slots = {}
+    members = {}
+    for (s, d) in sorted(via):
+        m = via[s, d]
+        if d not in slots.setdefault(m, []):
+            slots[m].append(d)
+        members.setdefault(d, [m]).append(s)
+    for d in members:
+        members[d].sort()
+
+    def farsem(s, d):
+        hosts = sorted({topo.host(cores[a]) for a in R if a != d and ok(a, d) and not near(a, d)})
+        return "far%d" % hosts.index(topo.host(cores[s]))
+
+    def direct(s, d, e0, ne):
+        return dict(dst=d, e0=e0, ne=ne, sem="near" if near(s, d) else farsem(s, d),
+                    sb="xs", sc=B * d, db="land", dc=B * s, w=B)
+
+    calls = {}
+    for j in R:
+        diag = [d for d in R if (j, d) in via]
+        mine = slots.get(j, [])
+        far = [d for d in R if d != j and ok(j, d) and not near(j, d) and d not in mine]
+        nr = [d for d in R if d != j and near(j, d)]
+        if diag:
+            first = []
+            for i, d in enumerate(diag):
+                m = via[j, d]
+                k = slots[m].index(d)
+                first.append(dict(dst=m, e0=2 * i, ne=2, sem="f%d" % k, sb="xs", sc=B * d,
+                                  db="fw%d" % k, dc=B * members[d].index(j), w=B))
+            second = [direct(j, d, 2 * i, 2) for i, d in enumerate(far)]
+            second += [direct(j, d, 2 * len(far) + i, 1) for i, d in enumerate(nr)]
+            calls[j] = [([("ldx", 16)], first), ([("ldy", 16)], second)]
+        else:
+            calls[j] = [([("ldx", 16)], [direct(j, d, 2 * i, 2) for i, d in enumerate(far)]),
+                        ([], [direct(j, d, 4 * i, 4) for i, d in enumerate(nr)]),
+                        (None, [dict(dst=d, e0=4 * k, ne=4, sem="rel", sb="fw%d" % k, sc=0, db="rl", dc=0,
+                                     w=B * len(members[d])) for k, d in enumerate(mine)])]
+    arrive = {j: {} for j in R}
+    for j in R:
+        for _, trs in calls[j]:
+            for t in trs:
+                arrive[t["dst"]][t["sem"]] = arrive[t["dst"]].get(t["sem"], 0) + t["ne"]
+    return dict(via=via, slots=slots, members=members, calls=calls, arrive=arrive, near=near, ok=ok)
+
+
+def rank_program(g, core, T, topo):
+    me = T.rank_of(core)
+    if me is None:
+        return
+    cores = list(T.cores)
+    R = range(len(cores))
+    P = _plan(cores, topo)
+    arrive, members, mine = P["arrive"][me], P["members"], P["slots"].get(me, [])
+    diag = [d for d in R if (me, d) in P["via"]]
+    sem = T.sem
+
+    nldy = 0
+    if diag:
+        lo, hi = B * diag[0], B * (diag[-1] + 1)
+        g.sync.dma_start(T.xs[:, lo:hi], T.x[:, lo:hi]).then_inc(sem.ldx, 16)
+        for run in _runs([d for d in R if d not in diag], lambda d: d):
+            a, b = B * run[0], B * (run[-1] + 1)
+            g.scalar.dma_start(T.xs[:, a:b], T.x[:, a:b]).then_inc(sem.ldy, 16)
+            nldy += 16
+        own_ld = ("ldy", nldy)
+    else:
+        g.sync.dma_start(T.xs[:, :], T.x[:, :]).then_inc(sem.ldx, 16)
+        for k, d in enumerate(mine):
+            p = B * members[d].index(me)
+            g.scalar.dma_start(T["fw%d" % k][:, p:p + B], T.x[:, B * d:B * d + B]).then_inc(sem.ldy, 16)
+            nldy += 16
+        own_ld = ("ldx", 16)
+    g.sync.dma_start(T.ws[:, :], T.w[:, :]).then_inc(sem.ldw, 16)
+
+    sent = 0
+    for waits, trs in P["calls"][me]:
+        if waits is None:
+            waits = [("ldy", nldy)] + [("f%d" % k, arrive["f%d" % k]) for k in range(len(mine))]
+        for s, v in waits:
+            g.wait_ge(sem[s], nldy if s == "ldy" else v)
+        fused = []
+        for t in trs:
+            dst = cores[t["dst"]]
+            engs = [b for b in range(16) if (topo.mask(core, dst) >> b) & 1]
+            mask = sum(1 << b for b in engs[t["e0"]:t["e0"] + t["ne"]])
+            rid, pid = topo.addr(dst, core)
+            fused.append(RemoteDMATransfer(dst_ids=[DstId(rid=rid, pnc=pid)], dma_engine_mask=mask, remote_sem=sem[t["sem"]],
+                                           src=T[t["sb"]][:, t["sc"]:t["sc"] + t["w"]],
+                                           dst=T[t["db"]][:, t["dc"]:t["dc"] + t["w"]]))
+            sent += t["ne"]
+        g.remote_dma_fused(fused, local_sem=sem.sent)
+
+    def landed(name):
+        return [(j, "land", B * j) for j in R for _, trs in P["calls"][j] for t in trs
+                if t["dst"] == me and t["sem"] == name]
+
+    groups = [([("ldw", 16), own_ld], [(me, "xs", B * me)])]
+    if diag:
+        order = ["far0", "near", "rel"]
+        stores = [((0, 2), g.scalar), ((1, 3), g.sync)]
+    else:
+        order = ["near", "far0", "far1"]
+        stores = [((0, 1), g.scalar), ((2,), g.sync), ((3,), g.scalar)]
+    for name in order:
+        blocks = [(j, "rl", B * p) for p, j in enumerate(members[me])] if name == "rel" else landed(name)
+        groups.append(([(name, arrive[name])], blocks))
+
+    ncopies = []
+    for gi, (waits, blocks) in enumerate(groups):
+        ps, mm, cp = T["ps%d" % gi], sem["mm%d" % gi], sem["cp%d" % gi]
+        pos = [(p,) + blk for p, blk in enumerate(blocks)]
+        for s, v in waits:
+            g.tensor.wait_ge(sem[s], v)
+        mruns = _runs(pos, lambda e: e[3] // B)
+        for run in mruns:
+            p, _, buf, col = run[0]
+            n = B * len(run)
+            g.tensor.matmul(ps[0:F, B * p:B * p + n], T.ws[:, :], T[buf][:, col:col + n], True, True).then_inc(mm, 1)
+        g.vector.wait_ge(mm, len(mruns))
+        cruns = _runs(pos, lambda e: e[1])
+        for run in cruns:
+            p, j = run[0][0], run[0][1]
+            n = B * len(run)
+            g.vector.tensor_copy(T.yb[0:F, B * j:B * j + n], ps[0:F, B * p:B * p + n]).then_inc(cp, 1)
+        ncopies.append(len(cruns))
+
+    for si, (gis, q) in enumerate(stores):
+        js = sorted(j for gi in gis for (j, _, _) in groups[gi][1])
+        assert js == list(range(js[0], js[-1] + 1))
+        for gi in gis:
+            q.wait_ge(sem["cp%d" % gi], ncopies[gi])
+        a, b = B * js[0], B * (js[-1] + 1)
+        q.dma_start(T.y[:, a:b], T.yb[0:F, a:b]).then_inc(sem["st%d" % si], 16)
+    for si, (_, q) in enumerate(stores):
+        q.wait_ge(sem["st%d" % si], 16)
+    g.wait_ge(sem.sent, sent)

@@ -3,7 +3,9 @@ from concourse.bass import DstId, RemoteDMATransfer
 B = 64
 F = 64
 NB = 9
-SLOT = 4
+DIAG8 = False
+RELAY2 = None
+SLOT = 3
 
 SCRATCH = {
     "xs": ("sbuf", [128, NB * B], "bfloat16"),
@@ -53,9 +55,7 @@ def _plan(cores, topo):
         m = via[s, d]
         if d not in slots.setdefault(m, []):
             slots[m].append(d)
-        members.setdefault(d, [m]).append(s)
-    for d in members:
-        members[d].sort()
+        members.setdefault(d, []).append(s)
 
     def farsem(s, d):
         hosts = sorted({topo.host(cores[a]) for a in R if a != d and ok(a, d) and not near(a, d)})
@@ -69,7 +69,7 @@ def _plan(cores, topo):
     for j in R:
         diag = [d for d in R if (j, d) in via]
         mine = slots.get(j, [])
-        far = [d for d in R if d != j and ok(j, d) and not near(j, d) and d not in mine]
+        far = [d for d in R if d != j and ok(j, d) and not near(j, d)]
         nr = [d for d in R if d != j and near(j, d)]
         if diag:
             first = []
@@ -80,18 +80,29 @@ def _plan(cores, topo):
                                   db="fw%d" % k, dc=B * members[d].index(j), w=B))
             second = [direct(j, d, 2 * i, 2) for i, d in enumerate(far)]
             second += [direct(j, d, 2 * len(far) + i, 1) for i, d in enumerate(nr)]
-            calls[j] = [([("ldx", 16)], first), ([("ldy", 16)], second)]
+            calls[j] = [(["ldx"], first), (["ldy"], second)]
+            if DIAG8:
+                for i, t in enumerate(first):
+                    t["e0"], t["ne"] = (4 * i, 4) if i < 2 else (0, 8)
+                rest = far + nr
+                calls[j] = [(["ldx"], first[:2]), ([], first[2:]),
+                            (["ldy"], [direct(j, d, 2 * i, 2) for i, d in enumerate(rest[:4])]),
+                            ([], [direct(j, d, 0, 8) for d in rest[4:]])]
         else:
-            calls[j] = [([("ldx", 16)], [direct(j, d, 2 * i, 2) for i, d in enumerate(far)]),
-                        ([], [direct(j, d, 4 * i, 4) for i, d in enumerate(nr)]),
-                        (None, [dict(dst=d, e0=4 * k, ne=4, sem="rel", sb="fw%d" % k, sc=0, db="rl", dc=0,
-                                     w=B * len(members[d])) for k, d in enumerate(mine)])]
+            def slot(k, e0, ne):
+                return dict(dst=mine[k], e0=e0, ne=ne, sem="rel", sb="fw%d" % k, sc=0, db="rl", dc=0,
+                            w=B * len(members[mine[k]]))
+            calls[j] = [(["ldx"], [direct(j, d, i, 1) for i, d in enumerate(far + nr)])]
+            if RELAY2 is None:
+                calls[j].append((["f%d" % k for k in range(len(mine))], [slot(k, 4 * k, 4) for k in range(len(mine))]))
+            else:
+                calls[j] += [(["f%d" % k], [slot(k, 0, 8)]) for k in RELAY2]
     arrive = {j: {} for j in R}
     for j in R:
         for _, trs in calls[j]:
             for t in trs:
                 arrive[t["dst"]][t["sem"]] = arrive[t["dst"]].get(t["sem"], 0) + t["ne"]
-    return dict(via=via, slots=slots, members=members, calls=calls, arrive=arrive, near=near, ok=ok)
+    return dict(via=via, slots=slots, members=members, calls=calls, arrive=arrive)
 
 
 def rank_program(g, core, T, topo):
@@ -101,34 +112,29 @@ def rank_program(g, core, T, topo):
     cores = list(T.cores)
     R = range(len(cores))
     P = _plan(cores, topo)
-    arrive, members, mine = P["arrive"][me], P["members"], P["slots"].get(me, [])
+    arrive, members = dict(P["arrive"][me]), P["members"]
     diag = [d for d in R if (me, d) in P["via"]]
     sem = T.sem
 
-    nldy = 0
+    arrive["ldx"] = arrive["ldw"] = 16
     if diag:
         lo, hi = B * diag[0], B * (diag[-1] + 1)
         g.sync.dma_start(T.xs[:, lo:hi], T.x[:, lo:hi]).then_inc(sem.ldx, 16)
+        arrive["ldy"] = 0
         for run in _runs([d for d in R if d not in diag], lambda d: d):
             a, b = B * run[0], B * (run[-1] + 1)
-            g.scalar.dma_start(T.xs[:, a:b], T.x[:, a:b]).then_inc(sem.ldy, 16)
-            nldy += 16
-        own_ld = ("ldy", nldy)
+            g.sync.dma_start(T.xs[:, a:b], T.x[:, a:b]).then_inc(sem.ldy, 16)
+            arrive["ldy"] += 16
+        own_ld = "ldy"
     else:
         g.sync.dma_start(T.xs[:, :], T.x[:, :]).then_inc(sem.ldx, 16)
-        for k, d in enumerate(mine):
-            p = B * members[d].index(me)
-            g.scalar.dma_start(T["fw%d" % k][:, p:p + B], T.x[:, B * d:B * d + B]).then_inc(sem.ldy, 16)
-            nldy += 16
-        own_ld = ("ldx", 16)
-    g.sync.dma_start(T.ws[:, :], T.w[:, :]).then_inc(sem.ldw, 16)
+        own_ld = "ldx"
+    g.scalar.dma_start(T.ws[:, :], T.w[:, :]).then_inc(sem.ldw, 16)
 
     sent = 0
     for waits, trs in P["calls"][me]:
-        if waits is None:
-            waits = [("ldy", nldy)] + [("f%d" % k, arrive["f%d" % k]) for k in range(len(mine))]
-        for s, v in waits:
-            g.wait_ge(sem[s], nldy if s == "ldy" else v)
+        for s in waits:
+            g.wait_ge(sem[s], arrive[s])
         fused = []
         for t in trs:
             dst = cores[t["dst"]]
@@ -145,23 +151,23 @@ def rank_program(g, core, T, topo):
         return [(j, "land", B * j) for j in R for _, trs in P["calls"][j] for t in trs
                 if t["dst"] == me and t["sem"] == name]
 
-    groups = [([("ldw", 16), own_ld], [(me, "xs", B * me)])]
+    groups = [(["ldw", own_ld], [(me, "xs", B * me)])]
     if diag:
         order = ["far0", "near", "rel"]
-        stores = [((0, 2), g.scalar), ((1, 3), g.sync)]
+        stores = [((1,), g.scalar), ((0, 2), g.scalar), ((3,), g.sync)]
     else:
         order = ["near", "far0", "far1"]
         stores = [((0, 1), g.scalar), ((2,), g.sync), ((3,), g.scalar)]
     for name in order:
         blocks = [(j, "rl", B * p) for p, j in enumerate(members[me])] if name == "rel" else landed(name)
-        groups.append(([(name, arrive[name])], blocks))
+        groups.append(([name], blocks))
 
     ncopies = []
     for gi, (waits, blocks) in enumerate(groups):
         ps, mm, cp = T["ps%d" % gi], sem["mm%d" % gi], sem["cp%d" % gi]
         pos = [(p,) + blk for p, blk in enumerate(blocks)]
-        for s, v in waits:
-            g.tensor.wait_ge(sem[s], v)
+        for s in waits:
+            g.tensor.wait_ge(sem[s], arrive[s])
         mruns = _runs(pos, lambda e: e[3] // B)
         for run in mruns:
             p, _, buf, col = run[0]

@@ -3,16 +3,15 @@ from concourse.bass import DstId, RemoteDMATransfer
 B = 64
 F = 64
 NB = 9
-DIAG8 = False
-RELAY2 = None
+HOSTS = 4
 SLOT = 3
+KR = 4
 
 SCRATCH = {
     "xs": ("sbuf", [128, NB * B], "bfloat16"),
     "ws": ("sbuf", [128, F], "bfloat16"),
     "land": ("sbuf", [128, NB * B], "bfloat16"),
-    "fw0": ("sbuf", [128, SLOT * B], "bfloat16"),
-    "fw1": ("sbuf", [128, SLOT * B], "bfloat16"),
+    "fw0": ("sbuf", [128, B], "bfloat16"),
     "rl": ("sbuf", [128, SLOT * B], "bfloat16"),
     "yb": ("sbuf", [128, NB * B], "bfloat16"),
     "ps0": ("psum", [128, 512], "float32"),
@@ -20,7 +19,7 @@ SCRATCH = {
     "ps2": ("psum", [128, 512], "float32"),
     "ps3": ("psum", [128, 512], "float32"),
 }
-SEMAPHORES = ["ldx", "ldy", "ldw", "sent", "near", "far0", "far1", "f0", "f1", "rel",
+SEMAPHORES = ["ldx", "ldy", "ldw", "sent", "near", "far0", "far1", "f0", "rel",
               "mm0", "mm1", "mm2", "mm3", "cp0", "cp1", "cp2", "cp3", "st0", "st1", "st2"]
 
 
@@ -36,6 +35,7 @@ def _runs(items, key):
 
 def _plan(cores, topo):
     R = range(len(cores))
+    world = range(HOSTS * topo.CORES_PER_HOST)
 
     def ok(s, d):
         return topo.may_write(cores[s], cores[d])
@@ -43,78 +43,87 @@ def _plan(cores, topo):
     def near(s, d):
         return topo.host(cores[s]) == topo.host(cores[d])
 
-    via = {}
-    for s in R:
-        for d in R:
+    via, members, taken = {}, {}, set(cores)
+    for d in R:
+        for s in R:
             if s != d and not ok(s, d):
-                via[s, d] = [m for m in R if m != s and m != d and ok(s, m) and ok(m, d)
-                             and topo.chip(cores[m]) == topo.chip(cores[d])][0]
-    slots = {}
-    members = {}
-    for (s, d) in sorted(via):
-        m = via[s, d]
-        if d not in slots.setdefault(m, []):
-            slots[m].append(d)
-        members.setdefault(d, []).append(s)
+                c = [c for c in world if c not in taken
+                     and topo.same_plane(cores[s], c) and topo.may_write(cores[s], c) and topo.may_write(c, cores[d])
+                     and topo.chip(c) == topo.chip(cores[d])
+                     and topo.rack(topo.host(c)) != topo.rack(topo.host(cores[d]))
+                     and topo.die(c) == topo.die(cores[s])][0]
+                taken.add(c)
+                via[s, d] = c
+                members.setdefault(d, []).append(s)
 
     def farsem(s, d):
         hosts = sorted({topo.host(cores[a]) for a in R if a != d and ok(a, d) and not near(a, d)})
         return "far%d" % hosts.index(topo.host(cores[s]))
 
     def direct(s, d, e0, ne):
-        return dict(dst=d, e0=e0, ne=ne, sem="near" if near(s, d) else farsem(s, d),
+        return dict(dst=cores[d], frm=s, e0=e0, ne=ne, sem="near" if near(s, d) else farsem(s, d),
                     sb="xs", sc=B * d, db="land", dc=B * s, w=B)
 
     calls = {}
     for j in R:
         diag = [d for d in R if (j, d) in via]
-        mine = slots.get(j, [])
         far = [d for d in R if d != j and ok(j, d) and not near(j, d)]
         nr = [d for d in R if d != j and near(j, d)]
         if diag:
-            first = []
-            for i, d in enumerate(diag):
-                m = via[j, d]
-                k = slots[m].index(d)
-                first.append(dict(dst=m, e0=2 * i, ne=2, sem="f%d" % k, sb="xs", sc=B * d,
-                                  db="fw%d" % k, dc=B * members[d].index(j), w=B))
+            first = [dict(dst=via[j, d], frm=j, e0=2 * i, ne=2, sem="f0", sb="xs", sc=B * d, db="fw0", dc=0, w=B)
+                     for i, d in enumerate(diag)]
             second = [direct(j, d, 2 * i, 2) for i, d in enumerate(far)]
             second += [direct(j, d, 2 * len(far) + i, 1) for i, d in enumerate(nr)]
-            calls[j] = [(["ldx"], first), (["ldy"], second)]
-            if DIAG8:
-                for i, t in enumerate(first):
-                    t["e0"], t["ne"] = (4 * i, 4) if i < 2 else (0, 8)
-                rest = far + nr
-                calls[j] = [(["ldx"], first[:2]), ([], first[2:]),
-                            (["ldy"], [direct(j, d, 2 * i, 2) for i, d in enumerate(rest[:4])]),
-                            ([], [direct(j, d, 0, 8) for d in rest[4:]])]
+            calls[cores[j]] = [(["ldx"], first), (["ldy"], second)]
         else:
-            def slot(k, e0, ne):
-                return dict(dst=mine[k], e0=e0, ne=ne, sem="rel", sb="fw%d" % k, sc=0, db="rl", dc=0,
-                            w=B * len(members[mine[k]]))
-            calls[j] = [(["ldx"], [direct(j, d, i, 1) for i, d in enumerate(far + nr)])]
-            if RELAY2 is None:
-                calls[j].append((["f%d" % k for k in range(len(mine))], [slot(k, 4 * k, 4) for k in range(len(mine))]))
-            else:
-                calls[j] += [(["f%d" % k], [slot(k, 0, 8)]) for k in RELAY2]
-    arrive = {j: {} for j in R}
-    for j in R:
-        for _, trs in calls[j]:
+            calls[cores[j]] = [(["ldx"], [direct(j, d, i, 1) for i, d in enumerate(far + nr)])]
+    for (s, d), c in via.items():
+        calls[c] = [(["f0"], [dict(dst=cores[d], frm=s, e0=0, ne=KR, sem="rel", sb="fw0", sc=0,
+                                   db="rl", dc=B * members[d].index(s), w=B)])]
+    arrive = {}
+    for c in calls:
+        for _, trs in calls[c]:
             for t in trs:
-                arrive[t["dst"]][t["sem"]] = arrive[t["dst"]].get(t["sem"], 0) + t["ne"]
-    return dict(via=via, slots=slots, members=members, calls=calls, arrive=arrive)
+                a = arrive.setdefault(t["dst"], {})
+                a[t["sem"]] = a.get(t["sem"], 0) + t["ne"]
+    return dict(via=via, members=members, calls=calls, arrive=arrive)
+
+
+def _send(g, core, T, topo, calls, arrive):
+    sem, sent = T.sem, 0
+    for waits, trs in calls:
+        for s in waits:
+            g.wait_ge(sem[s], arrive[s])
+        fused = []
+        for t in trs:
+            dst = t["dst"]
+            engs = [b for b in range(16) if (topo.mask(core, dst) >> b) & 1]
+            mask = sum(1 << b for b in engs[t["e0"]:t["e0"] + t["ne"]])
+            rid, pid = topo.addr(dst, core)
+            fused.append(RemoteDMATransfer(dst_ids=[DstId(rid=rid, pnc=pid)], dma_engine_mask=mask, remote_sem=sem[t["sem"]],
+                                           src=T[t["sb"]][:, t["sc"]:t["sc"] + t["w"]],
+                                           dst=T[t["db"]][:, t["dc"]:t["dc"] + t["w"]]))
+            sent += t["ne"]
+        g.remote_dma_fused(fused, local_sem=sem.sent)
+    return sent
 
 
 def rank_program(g, core, T, topo):
-    me = T.rank_of(core)
-    if me is None:
-        return
     cores = list(T.cores)
-    R = range(len(cores))
     P = _plan(cores, topo)
-    arrive, members = dict(P["arrive"][me]), P["members"]
-    diag = [d for d in R if (me, d) in P["via"]]
+    if core not in P["calls"]:
+        return
+    me = T.rank_of(core)
+    arrive = dict(P["arrive"].get(core, {}))
     sem = T.sem
+    if me is None:
+        sent = _send(g, core, T, topo, P["calls"][core], arrive)
+        g.wait_ge(sem.sent, sent)
+        return
+
+    R = range(len(cores))
+    members = P["members"]
+    diag = [d for d in R if (me, d) in P["via"]]
 
     arrive["ldx"] = arrive["ldw"] = 16
     if diag:
@@ -131,25 +140,11 @@ def rank_program(g, core, T, topo):
         own_ld = "ldx"
     g.scalar.dma_start(T.ws[:, :], T.w[:, :]).then_inc(sem.ldw, 16)
 
-    sent = 0
-    for waits, trs in P["calls"][me]:
-        for s in waits:
-            g.wait_ge(sem[s], arrive[s])
-        fused = []
-        for t in trs:
-            dst = cores[t["dst"]]
-            engs = [b for b in range(16) if (topo.mask(core, dst) >> b) & 1]
-            mask = sum(1 << b for b in engs[t["e0"]:t["e0"] + t["ne"]])
-            rid, pid = topo.addr(dst, core)
-            fused.append(RemoteDMATransfer(dst_ids=[DstId(rid=rid, pnc=pid)], dma_engine_mask=mask, remote_sem=sem[t["sem"]],
-                                           src=T[t["sb"]][:, t["sc"]:t["sc"] + t["w"]],
-                                           dst=T[t["db"]][:, t["dc"]:t["dc"] + t["w"]]))
-            sent += t["ne"]
-        g.remote_dma_fused(fused, local_sem=sem.sent)
+    sent = _send(g, core, T, topo, P["calls"][core], arrive)
 
     def landed(name):
-        return [(j, "land", B * j) for j in R for _, trs in P["calls"][j] for t in trs
-                if t["dst"] == me and t["sem"] == name]
+        return sorted((t["frm"], "land", B * t["frm"]) for c in P["calls"] for _, trs in P["calls"][c] for t in trs
+                      if t["dst"] == core and t["sem"] == name)
 
     groups = [(["ldw", own_ld], [(me, "xs", B * me)])]
     if diag:

@@ -6,21 +6,28 @@ NB = 9
 HOSTS = 4
 SLOT = 3
 KR = 4
+CH = 16
 
 SCRATCH = {
     "xs": ("sbuf", [128, NB * B], "bfloat16"),
     "ws": ("sbuf", [128, F], "bfloat16"),
     "land": ("sbuf", [128, NB * B], "bfloat16"),
-    "fw0": ("sbuf", [128, B], "bfloat16"),
+    "pa": ("dram", [SLOT, 128, CH], "bfloat16"),
+    "pb": ("dram", [SLOT, 128, B - CH], "bfloat16"),
+    "qa": ("dram", [1, 128, CH], "bfloat16"),
+    "qb": ("dram", [1, 128, B - CH], "bfloat16"),
     "rl": ("sbuf", [128, SLOT * B], "bfloat16"),
     "yb": ("sbuf", [128, NB * B], "bfloat16"),
     "ps0": ("psum", [128, 512], "float32"),
     "ps1": ("psum", [128, 512], "float32"),
     "ps2": ("psum", [128, 512], "float32"),
     "ps3": ("psum", [128, 512], "float32"),
+    "ps4": ("psum", [128, 512], "float32"),
+    "ps5": ("psum", [128, 512], "float32"),
 }
-SEMAPHORES = ["ldx", "ldy", "ldw", "sent", "near", "far0", "far1", "f0", "rel",
-              "mm0", "mm1", "mm2", "mm3", "cp0", "cp1", "cp2", "cp3", "st0", "st1", "st2"]
+SEMAPHORES = ["ldx", "ldz", "ldy", "ldw", "sent", "near", "far0", "far1", "f0", "f1", "rel0", "rel1", "rel2",
+              "mm0", "mm1", "mm2", "mm3", "mm4", "mm5", "cp0", "cp1", "cp2", "cp3", "cp4", "cp5",
+              "st0", "st1", "st2", "st3"]
 
 
 def _runs(items, key):
@@ -43,25 +50,42 @@ def _plan(cores, topo):
     def near(s, d):
         return topo.host(cores[s]) == topo.host(cores[d])
 
-    via, members, taken = {}, {}, set(cores)
-    for d in R:
-        for s in R:
-            if s != d and not ok(s, d):
-                c = [c for c in world if c not in taken
-                     and topo.same_plane(cores[s], c) and topo.may_write(cores[s], c) and topo.may_write(c, cores[d])
-                     and topo.chip(c) == topo.chip(cores[d])
-                     and topo.rack(topo.host(c)) != topo.rack(topo.host(cores[d]))
-                     and topo.die(c) == topo.die(cores[s])][0]
-                taken.add(c)
-                via[s, d] = c
-                members.setdefault(d, []).append(s)
+    def rk(c):
+        return topo.rack(topo.host(c))
+
+    def one_chip(a, b):
+        return topo.host(a) == topo.host(b) and topo.chip(a) == topo.chip(b)
+
+    refused = [(s, d) for d in R for s in R if s != d and not ok(s, d)]
+    via, members, taken, cabled = {}, {}, set(cores), set(cores)
+    for s, d in refused:
+        members.setdefault(d, []).append(s)
+    for s, d in refused:
+        S, D = cores[s], cores[d]
+        if topo.chip(S) != topo.chip(D):
+            cand = [c for c in world if c not in taken
+                    and topo.same_plane(S, c) and topo.may_write(S, c) and topo.may_write(c, D)
+                    and topo.chip(c) == topo.chip(D) and rk(c) != rk(D)
+                    and all(not one_chip(c, u) or abs(c - u) >= 2 for u in cabled)]
+            c = sorted(cand, key=lambda c: (topo.die(c) != topo.die(S), c))[0]
+            taken.add(c)
+            cabled.add(c)
+            via[s, d] = c
+    for s, d in refused:
+        S, D = cores[s], cores[d]
+        if topo.chip(S) == topo.chip(D):
+            c = [c for c in world if c not in taken
+                 and topo.chip(c) == topo.chip(S) and rk(c) != rk(S) and topo.may_write(S, c) and topo.may_write(c, D)
+                 and topo.same_plane(c, D) and topo.die(c) == topo.die(S)][0]
+            taken.add(c)
+            via[s, d] = c
 
     def farsem(s, d):
         hosts = sorted({topo.host(cores[a]) for a in R if a != d and ok(a, d) and not near(a, d)})
         return "far%d" % hosts.index(topo.host(cores[s]))
 
-    def direct(s, d, e0, ne):
-        return dict(dst=cores[d], frm=s, e0=e0, ne=ne, sem="near" if near(s, d) else farsem(s, d),
+    def direct(s, d, eng):
+        return dict(dst=cores[d], frm=s, eng=eng, sem="near" if near(s, d) else farsem(s, d),
                     sb="xs", sc=B * d, db="land", dc=B * s, w=B)
 
     calls = {}
@@ -70,22 +94,27 @@ def _plan(cores, topo):
         far = [d for d in R if d != j and ok(j, d) and not near(j, d)]
         nr = [d for d in R if d != j and near(j, d)]
         if diag:
-            first = [dict(dst=via[j, d], frm=j, e0=2 * i, ne=2, sem="f0", sb="xs", sc=B * d, db="fw0", dc=0, w=B)
+            heads = [dict(dst=via[j, d], frm=j, eng=[2 * i], sem="f0", sb="pa", sp=i, db="qa", dp=0)
                      for i, d in enumerate(diag)]
-            second = [direct(j, d, 2 * i, 2) for i, d in enumerate(far)]
-            second += [direct(j, d, 2 * len(far) + i, 1) for i, d in enumerate(nr)]
-            calls[cores[j]] = [(["ldx"], first), (["ldy"], second)]
+            rests = [dict(dst=via[j, d], frm=j, eng=[2 * i, 2 * i + 1], sem="f1", sb="pb", sp=i, db="qb", dp=0)
+                     for i, d in enumerate(diag)]
+            rest5 = [direct(j, d, [2 * i, 2 * i + 1]) for i, d in enumerate(far)]
+            rest5 += [direct(j, d, [2 * len(far) + i]) for i, d in enumerate(nr)]
+            calls[cores[j]] = [(["ldx"], heads), (["ldz"], rests), (["ldy"], rest5)]
         else:
-            calls[cores[j]] = [(["ldx"], [direct(j, d, i, 1) for i, d in enumerate(far + nr)])]
+            calls[cores[j]] = [(["ldx"], [direct(j, d, [i]) for i, d in enumerate(far + nr)])]
     for (s, d), c in via.items():
-        calls[c] = [(["f0"], [dict(dst=cores[d], frm=s, e0=0, ne=KR, sem="rel", sb="fw0", sc=0,
-                                   db="rl", dc=B * members[d].index(s), w=B)])]
+        p = members[d].index(s)
+        eng = [2 * i for i in range(KR)]
+        calls[c] = [(["f0"], [dict(dst=cores[d], frm=s, eng=eng, sem="rel%d" % p, sb="qa", sp=0, db="rl", dc=B * p, w=CH)]),
+                    (["f1"], [dict(dst=cores[d], frm=s, eng=eng, sem="rel%d" % p, sb="qb", sp=0,
+                                   db="rl", dc=B * p + CH, w=B - CH)])]
     arrive = {}
     for c in calls:
         for _, trs in calls[c]:
             for t in trs:
                 a = arrive.setdefault(t["dst"], {})
-                a[t["sem"]] = a.get(t["sem"], 0) + t["ne"]
+                a[t["sem"]] = a.get(t["sem"], 0) + len(t["eng"])
     return dict(via=via, members=members, calls=calls, arrive=arrive)
 
 
@@ -98,12 +127,13 @@ def _send(g, core, T, topo, calls, arrive):
         for t in trs:
             dst = t["dst"]
             engs = [b for b in range(16) if (topo.mask(core, dst) >> b) & 1]
-            mask = sum(1 << b for b in engs[t["e0"]:t["e0"] + t["ne"]])
+            mask = sum(1 << engs[i] for i in t["eng"])
             rid, pid = topo.addr(dst, core)
+            src = T[t["sb"]][t["sp"]] if "sp" in t else T[t["sb"]][:, t["sc"]:t["sc"] + t["w"]]
+            out = T[t["db"]][t["dp"]] if "dp" in t else T[t["db"]][:, t["dc"]:t["dc"] + t["w"]]
             fused.append(RemoteDMATransfer(dst_ids=[DstId(rid=rid, pnc=pid)], dma_engine_mask=mask, remote_sem=sem[t["sem"]],
-                                           src=T[t["sb"]][:, t["sc"]:t["sc"] + t["w"]],
-                                           dst=T[t["db"]][:, t["dc"]:t["dc"] + t["w"]]))
-            sent += t["ne"]
+                                           src=src, dst=out))
+            sent += len(t["eng"])
         g.remote_dma_fused(fused, local_sem=sem.sent)
     return sent
 
@@ -125,20 +155,28 @@ def rank_program(g, core, T, topo):
     members = P["members"]
     diag = [d for d in R if (me, d) in P["via"]]
 
-    arrive["ldx"] = arrive["ldw"] = 16
+    arrive["ldw"] = 16
     if diag:
-        lo, hi = B * diag[0], B * (diag[-1] + 1)
-        g.sync.dma_start(T.xs[:, lo:hi], T.x[:, lo:hi]).then_inc(sem.ldx, 16)
+        qs = [g.sync, g.scalar]
+        n = 0
+        for name, buf, lo, hi in (("ldx", "pa", 0, CH), ("ldz", "pb", CH, B)):
+            arrive[name] = 0
+            for i, d in enumerate(diag):
+                qs[n % 2].dma_start(T[buf][i], T.x[:, B * d + lo:B * d + hi]).then_inc(sem[name], 16)
+                arrive[name] += 16
+                n += 1
         arrive["ldy"] = 0
         for run in _runs([d for d in R if d not in diag], lambda d: d):
             a, b = B * run[0], B * (run[-1] + 1)
             g.sync.dma_start(T.xs[:, a:b], T.x[:, a:b]).then_inc(sem.ldy, 16)
             arrive["ldy"] += 16
+        g.scalar.dma_start(T.ws[:, :], T.w[:, :]).then_inc(sem.ldw, 16)
         own_ld = "ldy"
     else:
+        arrive["ldx"] = 16
         g.sync.dma_start(T.xs[:, :], T.x[:, :]).then_inc(sem.ldx, 16)
+        g.scalar.dma_start(T.ws[:, :], T.w[:, :]).then_inc(sem.ldw, 16)
         own_ld = "ldx"
-    g.scalar.dma_start(T.ws[:, :], T.w[:, :]).then_inc(sem.ldw, 16)
 
     sent = _send(g, core, T, topo, P["calls"][core], arrive)
 
@@ -148,14 +186,15 @@ def rank_program(g, core, T, topo):
 
     groups = [(["ldw", own_ld], [(me, "xs", B * me)])]
     if diag:
-        order = ["far0", "near", "rel"]
-        stores = [((1,), g.scalar), ((0, 2), g.scalar), ((3,), g.sync)]
+        for name in ("far0", "near"):
+            groups.append(([name], landed(name)))
+        for p, j in enumerate(members[me]):
+            groups.append((["rel%d" % p], [(j, "rl", B * p)]))
+        stores = [((1,), g.scalar), ((0, 2), g.scalar), ((3, 4), g.sync), ((5,), g.sync)]
     else:
-        order = ["near", "far0", "far1"]
+        for name in ("near", "far0", "far1"):
+            groups.append(([name], landed(name)))
         stores = [((0, 1), g.scalar), ((2,), g.sync), ((3,), g.scalar)]
-    for name in order:
-        blocks = [(j, "rl", B * p) for p, j in enumerate(members[me])] if name == "rel" else landed(name)
-        groups.append(([name], blocks))
 
     ncopies = []
     for gi, (waits, blocks) in enumerate(groups):

from concourse.bass import DstId, RemoteDMATransfer

B = 64
F = 64
NB = 9
HOSTS = 4
SLOT = 3
KR = 4
CH = 16

SCRATCH = {
    "xs": ("sbuf", [128, NB * B], "bfloat16"),
    "ws": ("sbuf", [128, F], "bfloat16"),
    "land": ("sbuf", [128, NB * B], "bfloat16"),
    "pa": ("dram", [SLOT, 128, CH], "bfloat16"),
    "pb": ("dram", [SLOT, 128, B - CH], "bfloat16"),
    "qa": ("dram", [1, 128, CH], "bfloat16"),
    "qb": ("dram", [1, 128, B - CH], "bfloat16"),
    "rl": ("sbuf", [128, SLOT * B], "bfloat16"),
    "yb": ("sbuf", [128, NB * B], "bfloat16"),
    "ps0": ("psum", [128, 512], "float32"),
    "ps1": ("psum", [128, 512], "float32"),
    "ps2": ("psum", [128, 512], "float32"),
    "ps3": ("psum", [128, 512], "float32"),
    "ps4": ("psum", [128, 512], "float32"),
    "ps5": ("psum", [128, 512], "float32"),
}
SEMAPHORES = ["ldx", "ldz", "ldy", "ldw", "sent", "near", "far0", "far1", "f0", "f1", "rel0", "rel1", "rel2",
              "mm0", "mm1", "mm2", "mm3", "mm4", "mm5", "cp0", "cp1", "cp2", "cp3", "cp4", "cp5",
              "st0", "st1", "st2", "st3"]


def _runs(items, key):
    out = []
    for it in items:
        if out and key(it) == key(out[-1][-1]) + 1:
            out[-1].append(it)
        else:
            out.append([it])
    return out


def _plan(cores, topo):
    R = range(len(cores))
    world = range(HOSTS * topo.CORES_PER_HOST)

    def ok(s, d):
        return topo.may_write(cores[s], cores[d])

    def near(s, d):
        return topo.host(cores[s]) == topo.host(cores[d])

    def rk(c):
        return topo.rack(topo.host(c))

    def one_chip(a, b):
        return topo.host(a) == topo.host(b) and topo.chip(a) == topo.chip(b)

    refused = [(s, d) for d in R for s in R if s != d and not ok(s, d)]
    via, members, taken, cabled = {}, {}, set(cores), set(cores)
    for s, d in refused:
        members.setdefault(d, []).append(s)
    for s, d in refused:
        S, D = cores[s], cores[d]
        if topo.chip(S) != topo.chip(D):
            cand = [c for c in world if c not in taken
                    and topo.same_plane(S, c) and topo.may_write(S, c) and topo.may_write(c, D)
                    and topo.chip(c) == topo.chip(D) and rk(c) != rk(D)
                    and all(not one_chip(c, u) or abs(c - u) >= 2 for u in cabled)]
            c = sorted(cand, key=lambda c: (topo.die(c) != topo.die(S), c))[0]
            taken.add(c)
            cabled.add(c)
            via[s, d] = c
    for s, d in refused:
        S, D = cores[s], cores[d]
        if topo.chip(S) == topo.chip(D):
            c = [c for c in world if c not in taken
                 and topo.chip(c) == topo.chip(S) and rk(c) != rk(S) and topo.may_write(S, c) and topo.may_write(c, D)
                 and topo.same_plane(c, D) and topo.die(c) == topo.die(S)][0]
            taken.add(c)
            via[s, d] = c

    def farsem(s, d):
        hosts = sorted({topo.host(cores[a]) for a in R if a != d and ok(a, d) and not near(a, d)})
        return "far%d" % hosts.index(topo.host(cores[s]))

    def direct(s, d, eng):
        return dict(dst=cores[d], frm=s, eng=eng, sem="near" if near(s, d) else farsem(s, d),
                    sb="xs", sc=B * d, db="land", dc=B * s, w=B)

    calls = {}
    for j in R:
        diag = [d for d in R if (j, d) in via]
        far = [d for d in R if d != j and ok(j, d) and not near(j, d)]
        nr = [d for d in R if d != j and near(j, d)]
        if diag:
            heads = [dict(dst=via[j, d], frm=j, eng=[2 * i], sem="f0", sb="pa", sp=i, db="qa", dp=0)
                     for i, d in enumerate(diag)]
            rests = [dict(dst=via[j, d], frm=j, eng=[2 * i, 2 * i + 1], sem="f1", sb="pb", sp=i, db="qb", dp=0)
                     for i, d in enumerate(diag)]
            rest5 = [direct(j, d, [2 * i, 2 * i + 1]) for i, d in enumerate(far)]
            rest5 += [direct(j, d, [2 * len(far) + i]) for i, d in enumerate(nr)]
            calls[cores[j]] = [(["ldx"], heads), (["ldz"], rests), (["ldy"], rest5)]
        else:
            calls[cores[j]] = [(["ldx"], [direct(j, d, [i]) for i, d in enumerate(far + nr)])]
    for (s, d), c in via.items():
        p = members[d].index(s)
        eng = [2 * i for i in range(KR)]
        calls[c] = [(["f0"], [dict(dst=cores[d], frm=s, eng=eng, sem="rel%d" % p, sb="qa", sp=0, db="rl", dc=B * p, w=CH)]),
                    (["f1"], [dict(dst=cores[d], frm=s, eng=eng, sem="rel%d" % p, sb="qb", sp=0,
                                   db="rl", dc=B * p + CH, w=B - CH)])]
    arrive = {}
    for c in calls:
        for _, trs in calls[c]:
            for t in trs:
                a = arrive.setdefault(t["dst"], {})
                a[t["sem"]] = a.get(t["sem"], 0) + len(t["eng"])
    return dict(via=via, members=members, calls=calls, arrive=arrive)


def _send(g, core, T, topo, calls, arrive):
    sem, sent = T.sem, 0
    for waits, trs in calls:
        for s in waits:
            g.wait_ge(sem[s], arrive[s])
        fused = []
        for t in trs:
            dst = t["dst"]
            engs = [b for b in range(16) if (topo.mask(core, dst) >> b) & 1]
            mask = sum(1 << engs[i] for i in t["eng"])
            rid, pid = topo.addr(dst, core)
            src = T[t["sb"]][t["sp"]] if "sp" in t else T[t["sb"]][:, t["sc"]:t["sc"] + t["w"]]
            out = T[t["db"]][t["dp"]] if "dp" in t else T[t["db"]][:, t["dc"]:t["dc"] + t["w"]]
            fused.append(RemoteDMATransfer(dst_ids=[DstId(rid=rid, pnc=pid)], dma_engine_mask=mask, remote_sem=sem[t["sem"]],
                                           src=src, dst=out))
            sent += len(t["eng"])
        g.remote_dma_fused(fused, local_sem=sem.sent)
    return sent


def rank_program(g, core, T, topo):
    cores = list(T.cores)
    P = _plan(cores, topo)
    if core not in P["calls"]:
        return
    me = T.rank_of(core)
    arrive = dict(P["arrive"].get(core, {}))
    sem = T.sem
    if me is None:
        sent = _send(g, core, T, topo, P["calls"][core], arrive)
        g.wait_ge(sem.sent, sent)
        return

    R = range(len(cores))
    members = P["members"]
    diag = [d for d in R if (me, d) in P["via"]]

    arrive["ldw"] = 16
    if diag:
        qs = [g.sync, g.scalar]
        n = 0
        for name, buf, lo, hi in (("ldx", "pa", 0, CH), ("ldz", "pb", CH, B)):
            arrive[name] = 0
            for i, d in enumerate(diag):
                qs[n % 2].dma_start(T[buf][i], T.x[:, B * d + lo:B * d + hi]).then_inc(sem[name], 16)
                arrive[name] += 16
                n += 1
        arrive["ldy"] = 0
        for run in _runs([d for d in R if d not in diag], lambda d: d):
            a, b = B * run[0], B * (run[-1] + 1)
            g.sync.dma_start(T.xs[:, a:b], T.x[:, a:b]).then_inc(sem.ldy, 16)
            arrive["ldy"] += 16
        g.scalar.dma_start(T.ws[:, :], T.w[:, :]).then_inc(sem.ldw, 16)
        own_ld = "ldy"
    else:
        arrive["ldx"] = 16
        g.sync.dma_start(T.xs[:, :], T.x[:, :]).then_inc(sem.ldx, 16)
        g.scalar.dma_start(T.ws[:, :], T.w[:, :]).then_inc(sem.ldw, 16)
        own_ld = "ldx"

    sent = _send(g, core, T, topo, P["calls"][core], arrive)

    def landed(name):
        return sorted((t["frm"], "land", B * t["frm"]) for c in P["calls"] for _, trs in P["calls"][c] for t in trs
                      if t["dst"] == core and t["sem"] == name)

    groups = [(["ldw", own_ld], [(me, "xs", B * me)])]
    if diag:
        for name in ("far0", "near"):
            groups.append(([name], landed(name)))
        for p, j in enumerate(members[me]):
            groups.append((["rel%d" % p], [(j, "rl", B * p)]))
        stores = [((1,), g.scalar), ((0, 2), g.scalar), ((3, 4), g.sync), ((5,), g.sync)]
    else:
        for name in ("near", "far0", "far1"):
            groups.append(([name], landed(name)))
        stores = [((0, 1), g.scalar), ((2,), g.sync), ((3,), g.scalar)]

    ncopies = []
    for gi, (waits, blocks) in enumerate(groups):
        ps, mm, cp = T["ps%d" % gi], sem["mm%d" % gi], sem["cp%d" % gi]
        pos = [(p,) + blk for p, blk in enumerate(blocks)]
        for s in waits:
            g.tensor.wait_ge(sem[s], arrive[s])
        mruns = _runs(pos, lambda e: e[3] // B)
        for run in mruns:
            p, _, buf, col = run[0]
            n = B * len(run)
            g.tensor.matmul(ps[0:F, B * p:B * p + n], T.ws[:, :], T[buf][:, col:col + n], True, True).then_inc(mm, 1)
        g.vector.wait_ge(mm, len(mruns))
        cruns = _runs(pos, lambda e: e[1])
        for run in cruns:
            p, j = run[0][0], run[0][1]
            n = B * len(run)
            g.vector.tensor_copy(T.yb[0:F, B * j:B * j + n], ps[0:F, B * p:B * p + n]).then_inc(cp, 1)
        ncopies.append(len(cruns))

    for si, (gis, q) in enumerate(stores):
        js = sorted(j for gi in gis for (j, _, _) in groups[gi][1])
        assert js == list(range(js[0], js[-1] + 1))
        for gi in gis:
            q.wait_ge(sem["cp%d" % gi], ncopies[gi])
        a, b = B * js[0], B * (js[-1] + 1)
        q.dma_start(T.y[:, a:b], T.yb[0:F, a:b]).then_inc(sem["st%d" % si], 16)
    for si, (_, q) in enumerate(stores):
        q.wait_ge(sem["st%d" % si], 16)
    g.wait_ge(sem.sent, sent)
